import numpy as np, ml_dtypes
CORES = [1,14,19,24,37,42,55,60,65,78,83,88,101,106,119,124]
N = 16
TK = 32
def setup_inputs(rng):
    return {"x": rng.standard_normal((N, 128, N * TK), dtype=np.float32).astype(ml_dtypes.bfloat16), "t": rng.standard_normal((N, 128, N * TK), dtype=np.float32).astype(ml_dtypes.bfloat16), "f1": (rng.standard_normal((N, 128, 128), dtype=np.float32) / 11).astype(ml_dtypes.bfloat16), "f2": (rng.standard_normal((N, 128, 128), dtype=np.float32) / 11).astype(ml_dtypes.bfloat16)}
def setup_inputs_big(rng):
    d = setup_inputs(rng)
    for k in ("x", "t", "f1", "f2"): d[k] = (d[k].astype(np.float32) * 1024.0).astype(d[k].dtype)
    return d
def setup_inputs_small(rng):
    d = setup_inputs(rng)
    for k in ("x", "t", "f1", "f2"): d[k] = (d[k].astype(np.float32) * (1 / 1024.0)).astype(d[k].dtype)
    return d
def reference(x, t, f1, f2):
    X, T, F1, F2 = x.astype(np.float64), t.astype(np.float64), f1.astype(np.float64), f2.astype(np.float64)
    y = np.zeros((N, 128, N * TK))
    for j in range(N):
        u = (F1[j].T @ X[j]) * T[j]
        for r in range(N):
            y[r][:, TK * j:TK * j + TK] = F2[r].T @ u[:, TK * r:TK * r + TK]
    return {"y": y.astype(ml_dtypes.bfloat16)}

@@ -1,0 +1,227 @@
+from concourse.bass import DstId, RemoteDMATransfer
+from concourse.mybir import AluOpType
+
+N, TK = 16, 32
+HB = N // 2
+CHUNKS = 1
+JPC = 4
+ON_TOT = 16
+ON_HIGH = False
+E_H = 4
+NSP = 0
+
+BF, F32 = "bfloat16", "float32"
+SCRATCH = {
+    "f1s": ("sbuf", [128, 128], BF),
+    "f2s": ("sbuf", [128, 128], BF),
+    "xs": ("sbuf", [128, HB, 2, TK], BF),
+    "ts": ("sbuf", [128, HB, 2, TK], BF),
+    "uc": ("sbuf", [128, HB, TK], BF),
+    "us": ("sbuf", [128, HB, TK], BF),
+    "hb": ("sbuf", [128, 2, TK], BF),
+    "lc": ("sbuf", [128, HB, TK], BF),
+    "ls": ("sbuf", [128, HB, TK], BF),
+    "ys": ("sbuf", [128, HB, 2, TK], BF),
+    "pc": ("psum", [128, N, TK], F32),
+    "pd": ("psum", [128, N, TK], F32),
+}
+SEMAPHORES = ["lf1", "lf2", "ur", "own", "got", "arrs", "arrc", "sent", "y1", "y2", "cp", "st", "o0", "o1", "o2"]
+for _c in range(CHUNKS):
+    SCRATCH["pa%d" % _c] = ("psum", [128, N, TK], F32)
+    SCRATCH["pb%d" % _c] = ("psum", [128, N, TK], F32)
+    SEMAPHORES += ["lx%d" % _c, "lt%d" % _c, "mc%d" % _c, "ms%d" % _c, "uc%d" % _c]
+
+
+def _eng(topo, src, dst):
+    m = topo.mask(src, dst)
+    return [e for e in range(m.bit_length()) if (m >> e) & 1]
+
+
+def _bits(es):
+    return sum(1 << e for e in es)
+
+
+def _pow2(n):
+    p = 1
+    while p * 2 <= n:
+        p *= 2
+    return p
+
+
+def _ranges(idx):
+    out = []
+    for i in sorted(idx):
+        if out and out[-1][1] == i:
+            out[-1][1] = i + 1
+        else:
+            out.append([i, i + 1])
+    return [tuple(r) for r in out]
+
+
+def _plan(T, topo):
+    cores = list(T.cores)
+    n = len(cores)
+    plan = []
+    for j, R in enumerate(cores):
+        ch = topo.chip(R)
+        same = [r for r in range(n) if r == j or topo.same_plane(ch, topo.chip(cores[r]))]
+        cross = [r for r in range(n) if r not in same]
+        par_c, par_s = cross[0] % 2, same[0] % 2
+        assert cross == [2 * i + par_c for i in range(HB)] and same == [2 * i + par_s for i in range(HB)]
+        chip = [k for k in range(topo.CORES_PER_CHIP * topo.CHIPS) if topo.chip(k) == ch]
+        away = lambda k: topo.die(k) != topo.die(R)
+        port = sorted([k for k in chip if all(topo.may_write(k, cores[r]) for r in cross)],
+                      key=lambda k: (away(k), k == R))
+        rest = sorted([k for k in chip if k not in port and k != R], key=away)
+        assert 2 * len(port) == HB
+        own = same.index(j)
+        jobs, direct = [], []
+        free = [i for i in range(0, HB, 2) if own not in (i, i + 1)]
+        off = []
+        for i, k in zip(range(0, HB, 2), port):
+            if k != R:
+                jobs.append((k, "uc", i, cross[i:i + 2]))
+            else:
+                direct += [("uc", i, cross[i]), ("uc", i + 1, cross[i + 1])]
+                s = sorted(free, key=lambda f: f // (HB // 2) != i // (HB // 2))[0]
+                free.remove(s)
+                jobs.append((rest.pop(0), "us", s, same[s:s + 2]))
+                off.append(s)
+        jobs.sort(key=lambda jb: jb[2] // (HB // CHUNKS))
+        for s in free[:NSP]:
+            jobs.append((rest.pop(), "us", s, same[s:s + 2]))
+            off.append(s)
+        direct += [("us", i, same[i]) for i in range(HB) if i != own and i not in off and i - 1 not in off]
+        far = _eng(topo, R, cores[cross[0]])
+        on = _eng(topo, R, jobs[0][0])
+        if ON_HIGH:
+            on = [e for e in on if e not in far] + [e for e in on if e in far]
+        calls = []
+        for a in range(0, len(jobs), JPC):
+            js = jobs[a:a + JPC]
+            per = _pow2(ON_TOT // len(js))
+            calls.append([(jb, on[k * per:(k + 1) * per]) for k, jb in enumerate(js)])
+        plan.append(dict(core=R, same=same, cross=cross, par_c=par_c, par_s=par_s, own=own, calls=calls,
+                         direct=direct, off=off, per_dir=_pow2(len(far) // len(direct))))
+    return plan
+
+
+def _send(g, T, topo, plan, j, core, items, per, local_sem):
+    trs = []
+    for k, (src, r) in enumerate(items):
+        P = plan[r]
+        dst = P["core"]
+        rid, pid, _ = topo.addr(dst)
+        if j in P["cross"]:
+            land, sem = T.lc[:, P["cross"].index(j), :], T.sem.arrc
+        else:
+            land, sem = T.ls[:, P["same"].index(j), :], T.sem.arrs
+        trs.append(RemoteDMATransfer(dst_ids=[DstId(rid=rid, pnc=pid)],
+                                     dma_engine_mask=_bits(_eng(topo, core, dst)[k * per:(k + 1) * per]),
+                                     remote_sem=sem, src=src, dst=land))
+    g.remote_dma_fused(trs, local_sem=local_sem)
+    return per * len(items)
+
+
+def rank_program(g, core, T, topo):
+    plan = _plan(T, topo)
+    S = T.sem
+    rank = T.rank_of(core)
+
+    if rank is None:
+        for j, P in enumerate(plan):
+            for call in P["calls"]:
+                for jb, es in call:
+                    if jb[0] == core:
+                        g.wait_ge(S.got, len(es))
+                        sent = _send(g, T, topo, plan, j, core,
+                                     [(T.hb[:, d, :], r) for d, r in enumerate(jb[3])], E_H, S.sent)
+                        g.wait_ge(S.sent, sent)
+        return
+
+    P = plan[rank]
+    pc, ps, own, off = P["par_c"], P["par_s"], P["own"], P["off"]
+    te, ve = g.tensor, g.vector
+    W = HB // CHUNKS
+    mult = AluOpType.mult
+
+    g.scalar.dma_start(out=T.f1s[:], in_=T.f1[:]).then_inc(S.lf1, 16)
+    for c in range(CHUNKS):
+        a, b = c * W, (c + 1) * W
+        g.sync.dma_start(out=T.xs[:, a:b, :, :], in_=T.x[:, 2 * TK * a:2 * TK * b]).then_inc(S["lx%d" % c], 16)
+        g.scalar.dma_start(out=T.ts[:, a:b, :, :], in_=T.t[:, 2 * TK * a:2 * TK * b]).then_inc(S["lt%d" % c], 16)
+    g.scalar.dma_start(out=T.f2s[:], in_=T.f2[:]).then_inc(S.lf2, 16)
+
+    te.wait_ge(S.lf1, 16)
+    for c in range(CHUNKS):
+        a, b = c * W, (c + 1) * W
+        te.wait_ge(S["lx%d" % c], 16)
+        te.matmul(out=T["pa%d" % c][:, 0:W, :], lhsT=T.f1s[:], rhs=T.xs[:, a:b, pc, :],
+                  start=True, stop=True).then_inc(S["mc%d" % c], 1)
+        te.matmul(out=T["pb%d" % c][:, 0:W, :], lhsT=T.f1s[:], rhs=T.xs[:, a:b, ps, :],
+                  start=True, stop=True).then_inc(S["ms%d" % c], 1)
+
+    def same_op(a, b, out, sem):
+        c = a // W
+        ve.tensor_tensor(out=out, in0=T["pb%d" % c][:, a - c * W:b - c * W, :], in1=T.ts[:, a:b, ps, :],
+                         op=mult).then_inc(sem, 1)
+
+    for c in range(CHUNKS):
+        a, b = c * W, (c + 1) * W
+        ve.wait_ge(S["lt%d" % c], 16)
+        ve.wait_ge(S["mc%d" % c], 1)
+        ve.tensor_tensor(out=T.uc[:, a:b, :], in0=T["pa%d" % c][:, 0:W, :], in1=T.ts[:, a:b, pc, :],
+                         op=mult).then_inc(S["uc%d" % c], 1)
+        ve.wait_ge(S["ms%d" % c], 1)
+        for k, i in enumerate(off):
+            if a <= i < b:
+                same_op(i, i + 2, T.us[:, i:i + 2, :], S["o%d" % k])
+    nr = 0
+    for c in range(CHUNKS):
+        for a, b in _ranges([i for i in range(c * W, (c + 1) * W) if i not in off and i - 1 not in off]):
+            same_op(a, b, T.us[:, a:b, :], S.ur)
+            nr += 1
+    same_op(own, own + 1, T.ls[:, own:own + 1, :], S.own)
+
+    sent = 0
+    seen = set()
+    for call in P["calls"]:
+        trs = []
+        for (h, buf, i, _), es in call:
+            need = "uc%d" % (i // W) if buf == "uc" else "o%d" % off.index(i)
+            if need not in seen:
+                seen.add(need)
+                g.wait_ge(S[need], 1)
+            rid, pid, _ = topo.addr(h)
+            trs.append(RemoteDMATransfer(dst_ids=[DstId(rid=rid, pnc=pid)], dma_engine_mask=_bits(es),
+                                         remote_sem=S.got, src=T[buf][:, i:i + 2, :], dst=T.hb[:]))
+            sent += len(es)
+        g.remote_dma_fused(trs, local_sem=S.sent)
+    for c in range(CHUNKS):
+        if "uc%d" % c not in seen:
+            g.wait_ge(S["uc%d" % c], 1)
+    g.wait_ge(S.ur, nr)
+    sent += _send(g, T, topo, plan, rank, core, [(T[buf][:, i, :], r) for buf, i, r in P["direct"]],
+                  P["per_dir"], S.sent)
+
+    exp = {"same": 0, "cross": 0}
+    for j, Q in enumerate(plan):
+        if j != rank:
+            cls = "cross" if j in P["cross"] else "same"
+            exp[cls] += sum(E_H for call in Q["calls"] for jb, es in call if rank in jb[3])
+            exp[cls] += sum(Q["per_dir"] for d in Q["direct"] if d[2] == rank)
+
+    te.wait_ge(S.lf2, 16)
+    te.wait_ge(S.own, 1)
+    te.wait_ge(S.arrs, exp["same"])
+    te.matmul(out=T.pc[:, 0:HB, :], lhsT=T.f2s[:], rhs=T.ls[:], start=True, stop=True).then_inc(S.y1, 1)
+    te.wait_ge(S.arrc, exp["cross"])
+    te.matmul(out=T.pd[:, 0:HB, :], lhsT=T.f2s[:], rhs=T.lc[:], start=True, stop=True).then_inc(S.y2, 1)
+    ve.wait_ge(S.y1, 1)
+    ve.tensor_copy(out=T.ys[:, :, ps, :], in_=T.pc[:, 0:HB, :]).then_inc(S.cp, 1)
+    ve.wait_ge(S.y2, 1)
+    ve.tensor_copy(out=T.ys[:, :, pc, :], in_=T.pd[:, 0:HB, :]).then_inc(S.cp, 1)
+    g.sync.wait_ge(S.cp, 2)
+    g.sync.dma_start(out=T.y[:], in_=T.ys[:]).then_inc(S.st, 16)
+    g.sync.wait_ge(S.st, 16)
+    g.wait_ge(S.sent, sent)

@@ -3,12 +3,8 @@ from concourse.mybir import AluOpType
 
 N, TK = 16, 32
 HB = N // 2
-CHUNKS = 1
-JPC = 4
-ON_TOT = 16
-ON_HIGH = False
-E_H = 4
-NSP = 0
+CH = 2
+W = HB // CH
 
 BF, F32 = "bfloat16", "float32"
 SCRATCH = {
@@ -18,18 +14,20 @@ SCRATCH = {
     "ts": ("sbuf", [128, HB, 2, TK], BF),
     "uc": ("sbuf", [128, HB, TK], BF),
     "us": ("sbuf", [128, HB, TK], BF),
-    "hb": ("sbuf", [128, 2, TK], BF),
-    "lc": ("sbuf", [128, HB, TK], BF),
-    "ls": ("sbuf", [128, HB, TK], BF),
+    "hb0": ("sbuf", [128, TK], BF),
+    "hb1": ("sbuf", [128, TK], BF),
+    "land": ("sbuf", [128, HB, 2, TK], BF),
     "ys": ("sbuf", [128, HB, 2, TK], BF),
+    "pe": ("psum", [128, HB, 2, TK], F32),
     "pc": ("psum", [128, N, TK], F32),
     "pd": ("psum", [128, N, TK], F32),
 }
-SEMAPHORES = ["lf1", "lf2", "ur", "own", "got", "arrs", "arrc", "sent", "y1", "y2", "cp", "st", "o0", "o1", "o2"]
-for _c in range(CHUNKS):
+SEMAPHORES = ["lf1", "lf2", "own", "arre", "arrs", "arrc", "sent", "y0", "y1", "y2", "cpe", "cp", "st"]
+for _c in range(CH):
     SCRATCH["pa%d" % _c] = ("psum", [128, N, TK], F32)
     SCRATCH["pb%d" % _c] = ("psum", [128, N, TK], F32)
-    SEMAPHORES += ["lx%d" % _c, "lt%d" % _c, "mc%d" % _c, "ms%d" % _c, "uc%d" % _c]
+    SEMAPHORES += ["lx%d" % _c, "lt%d" % _c, "mc%d" % _c, "ms%d" % _c, "uc%d" % _c, "ur%d" % _c, "o%d" % _c,
+                   "got%d" % _c]
 
 
 def _eng(topo, src, dst):
@@ -73,54 +71,51 @@ def _plan(T, topo):
         port = sorted([k for k in chip if all(topo.may_write(k, cores[r]) for r in cross)],
                       key=lambda k: (away(k), k == R))
         rest = sorted([k for k in chip if k not in port and k != R], key=away)
-        assert 2 * len(port) == HB
+        assert len(port) == W
         own = same.index(j)
-        jobs, direct = [], []
-        free = [i for i in range(0, HB, 2) if own not in (i, i + 1)]
+        first = own // W
+        half = [first] + [h for h in range(CH) if h != first]
+        jobs = []
+        direct = [[] for _ in range(CH)]
         off = []
-        for i, k in zip(range(0, HB, 2), port):
-            if k != R:
-                jobs.append((k, "uc", i, cross[i:i + 2]))
+        for k, h in enumerate(port):
+            if h != R:
+                jobs.append((h, [("uc", k + c * W, cross[k + c * W]) for c in half]))
             else:
-                direct += [("uc", i, cross[i]), ("uc", i + 1, cross[i + 1])]
-                s = sorted(free, key=lambda f: f // (HB // 2) != i // (HB // 2))[0]
-                free.remove(s)
-                jobs.append((rest.pop(0), "us", s, same[s:s + 2]))
-                off.append(s)
-        jobs.sort(key=lambda jb: jb[2] // (HB // CHUNKS))
-        for s in free[:NSP]:
-            jobs.append((rest.pop(), "us", s, same[s:s + 2]))
-            off.append(s)
-        direct += [("us", i, same[i]) for i in range(HB) if i != own and i not in off and i - 1 not in off]
+                for p, c in enumerate(half):
+                    direct[p].append(("uc", k + c * W, cross[k + c * W]))
+                    off.append([i for i in range(c * W, (c + 1) * W) if i != own][0])
+                jobs.append((rest.pop(0), [("us", s, same[s]) for s in off]))
+        for p, c in enumerate(half):
+            direct[p] += [("us", i, same[i]) for i in range(c * W, (c + 1) * W) if i != own and i not in off]
         far = _eng(topo, R, cores[cross[0]])
         on = _eng(topo, R, jobs[0][0])
-        if ON_HIGH:
-            on = [e for e in on if e not in far] + [e for e in on if e in far]
-        calls = []
-        for a in range(0, len(jobs), JPC):
-            js = jobs[a:a + JPC]
-            per = _pow2(ON_TOT // len(js))
-            calls.append([(jb, on[k * per:(k + 1) * per]) for k, jb in enumerate(js)])
-        plan.append(dict(core=R, same=same, cross=cross, par_c=par_c, par_s=par_s, own=own, calls=calls,
-                         direct=direct, off=off, per_dir=_pow2(len(far) // len(direct))))
+        high = [e for e in on if e not in far] or on
+        pools = [on, high]
+        plan.append(dict(core=R, same=same, cross=cross, par_c=par_c, par_s=par_s, own=own, jobs=jobs,
+                         direct=direct, off=off, pools=pools, half=half,
+                         per_on=[_pow2(len(p) // len(jobs)) for p in pools],
+                         per_dir=[_pow2(len(far) // len(d)) for d in direct]))
     return plan
 
 
-def _send(g, T, topo, plan, j, core, items, per, local_sem):
+def _send(g, T, topo, plan, j, core, items, per, local_sem, wave):
     trs = []
     for k, (src, r) in enumerate(items):
         P = plan[r]
         dst = P["core"]
         rid, pid, _ = topo.addr(dst)
-        if j in P["cross"]:
-            land, sem = T.lc[:, P["cross"].index(j), :], T.sem.arrc
-        else:
-            land, sem = T.ls[:, P["same"].index(j), :], T.sem.arrs
+        land = T.land[:, j // 2, j % 2, :]
+        sem = T.sem.arre if wave == 0 else T.sem.arrc if j in P["cross"] else T.sem.arrs
         trs.append(RemoteDMATransfer(dst_ids=[DstId(rid=rid, pnc=pid)],
                                      dma_engine_mask=_bits(_eng(topo, core, dst)[k * per:(k + 1) * per]),
                                      remote_sem=sem, src=src, dst=land))
     g.remote_dma_fused(trs, local_sem=local_sem)
     return per * len(items)
+
+
+def _relay_engines(topo, plan, helper, r):
+    return _pow2(len(_eng(topo, helper, plan[r]["core"])))
 
 
 def rank_program(g, core, T, topo):
@@ -130,98 +125,108 @@ def rank_program(g, core, T, topo):
 
     if rank is None:
         for j, P in enumerate(plan):
-            for call in P["calls"]:
-                for jb, es in call:
-                    if jb[0] == core:
-                        g.wait_ge(S.got, len(es))
-                        sent = _send(g, T, topo, plan, j, core,
-                                     [(T.hb[:, d, :], r) for d, r in enumerate(jb[3])], E_H, S.sent)
-                        g.wait_ge(S.sent, sent)
+            for h, pieces in P["jobs"]:
+                if h == core:
+                    sent = 0
+                    for c, (_, _, r) in enumerate(pieces):
+                        g.wait_ge(S["got%d" % c], P["per_on"][c])
+                        sent += _send(g, T, topo, plan, j, core, [(T["hb%d" % c][:], r)],
+                                      _relay_engines(topo, plan, core, r), S.sent, c)
+                    g.wait_ge(S.sent, sent)
         return
 
     P = plan[rank]
-    pc, ps, own, off = P["par_c"], P["par_s"], P["own"], P["off"]
+    pc, ps, own, off, half = P["par_c"], P["par_s"], P["own"], P["off"], P["half"]
     te, ve = g.tensor, g.vector
-    W = HB // CHUNKS
     mult = AluOpType.mult
+    span = [(h * W, (h + 1) * W) for h in half]
+    (a0, b0), (a1, b1) = span
+    w = 2 * TK
 
+    g.sync.dma_start(out=T.xs[:, a0:b0, :, :], in_=T.x[:, w * a0:w * b0]).then_inc(S.lx0, 16)
     g.scalar.dma_start(out=T.f1s[:], in_=T.f1[:]).then_inc(S.lf1, 16)
-    for c in range(CHUNKS):
-        a, b = c * W, (c + 1) * W
-        g.sync.dma_start(out=T.xs[:, a:b, :, :], in_=T.x[:, 2 * TK * a:2 * TK * b]).then_inc(S["lx%d" % c], 16)
-        g.scalar.dma_start(out=T.ts[:, a:b, :, :], in_=T.t[:, 2 * TK * a:2 * TK * b]).then_inc(S["lt%d" % c], 16)
+    g.scalar.dma_start(out=T.ts[:, a0:b0, :, :], in_=T.t[:, w * a0:w * b0]).then_inc(S.lt0, 16)
+    g.scalar.dma_start(out=T.xs[:, a1:b1, :, :], in_=T.x[:, w * a1:w * b1]).then_inc(S.lx1, 16)
+    g.scalar.dma_start(out=T.ts[:, a1:b1, :, :], in_=T.t[:, w * a1:w * b1]).then_inc(S.lt1, 16)
     g.scalar.dma_start(out=T.f2s[:], in_=T.f2[:]).then_inc(S.lf2, 16)
 
     te.wait_ge(S.lf1, 16)
-    for c in range(CHUNKS):
-        a, b = c * W, (c + 1) * W
+    for c, (a, b) in enumerate(span):
         te.wait_ge(S["lx%d" % c], 16)
         te.matmul(out=T["pa%d" % c][:, 0:W, :], lhsT=T.f1s[:], rhs=T.xs[:, a:b, pc, :],
                   start=True, stop=True).then_inc(S["mc%d" % c], 1)
         te.matmul(out=T["pb%d" % c][:, 0:W, :], lhsT=T.f1s[:], rhs=T.xs[:, a:b, ps, :],
                   start=True, stop=True).then_inc(S["ms%d" % c], 1)
 
-    def same_op(a, b, out, sem):
-        c = a // W
-        ve.tensor_tensor(out=out, in0=T["pb%d" % c][:, a - c * W:b - c * W, :], in1=T.ts[:, a:b, ps, :],
+    def same_op(c, p, q, out, sem):
+        a = span[c][0]
+        ve.tensor_tensor(out=out, in0=T["pb%d" % c][:, p - a:q - a, :], in1=T.ts[:, p:q, ps, :],
                          op=mult).then_inc(sem, 1)
 
-    for c in range(CHUNKS):
-        a, b = c * W, (c + 1) * W
+    nr = [0] * CH
+    for c, (a, b) in enumerate(span):
         ve.wait_ge(S["lt%d" % c], 16)
         ve.wait_ge(S["mc%d" % c], 1)
         ve.tensor_tensor(out=T.uc[:, a:b, :], in0=T["pa%d" % c][:, 0:W, :], in1=T.ts[:, a:b, pc, :],
                          op=mult).then_inc(S["uc%d" % c], 1)
         ve.wait_ge(S["ms%d" % c], 1)
-        for k, i in enumerate(off):
-            if a <= i < b:
-                same_op(i, i + 2, T.us[:, i:i + 2, :], S["o%d" % k])
-    nr = 0
-    for c in range(CHUNKS):
-        for a, b in _ranges([i for i in range(c * W, (c + 1) * W) if i not in off and i - 1 not in off]):
-            same_op(a, b, T.us[:, a:b, :], S.ur)
-            nr += 1
-    same_op(own, own + 1, T.ls[:, own:own + 1, :], S.own)
+        if off:
+            same_op(c, off[c], off[c] + 1, T.us[:, off[c]:off[c] + 1, :], S["o%d" % c])
+        for p, q in _ranges([i for i in range(a, b) if i not in off]):
+            same_op(c, p, q, T.us[:, p:q, :], S["ur%d" % c])
+            nr[c] += 1
+    same_op(0, own, own + 1, T.land[:, own:own + 1, ps, :], S.own)
 
     sent = 0
-    seen = set()
-    for call in P["calls"]:
+    for c in range(CH):
+        g.wait_ge(S["uc%d" % c], 1)
+        if off:
+            g.wait_ge(S["o%d" % c], 1)
+        per, pool = P["per_on"][c], P["pools"][c]
         trs = []
-        for (h, buf, i, _), es in call:
-            need = "uc%d" % (i // W) if buf == "uc" else "o%d" % off.index(i)
-            if need not in seen:
-                seen.add(need)
-                g.wait_ge(S[need], 1)
+        for k, (h, pieces) in enumerate(P["jobs"]):
+            buf, i, _ = pieces[c]
             rid, pid, _ = topo.addr(h)
-            trs.append(RemoteDMATransfer(dst_ids=[DstId(rid=rid, pnc=pid)], dma_engine_mask=_bits(es),
-                                         remote_sem=S.got, src=T[buf][:, i:i + 2, :], dst=T.hb[:]))
-            sent += len(es)
+            trs.append(RemoteDMATransfer(dst_ids=[DstId(rid=rid, pnc=pid)],
+                                         dma_engine_mask=_bits(pool[k * per:(k + 1) * per]),
+                                         remote_sem=S["got%d" % c], src=T[buf][:, i, :], dst=T["hb%d" % c][:]))
+            sent += per
         g.remote_dma_fused(trs, local_sem=S.sent)
-    for c in range(CHUNKS):
-        if "uc%d" % c not in seen:
-            g.wait_ge(S["uc%d" % c], 1)
-    g.wait_ge(S.ur, nr)
-    sent += _send(g, T, topo, plan, rank, core, [(T[buf][:, i, :], r) for buf, i, r in P["direct"]],
-                  P["per_dir"], S.sent)
+        g.wait_ge(S["ur%d" % c], nr[c])
+        sent += _send(g, T, topo, plan, rank, core, [(T[buf][:, i, :], r) for buf, i, r in P["direct"][c]],
+                      P["per_dir"][c], S.sent, c)
 
-    exp = {"same": 0, "cross": 0}
+    exp = {"e": 0, "s": 0, "c": 0}
     for j, Q in enumerate(plan):
         if j != rank:
-            cls = "cross" if j in P["cross"] else "same"
-            exp[cls] += sum(E_H for call in Q["calls"] for jb, es in call if rank in jb[3])
-            exp[cls] += sum(Q["per_dir"] for d in Q["direct"] if d[2] == rank)
+            late = "c" if j in P["cross"] else "s"
+            for h, pieces in Q["jobs"]:
+                for c, pcs in enumerate(pieces):
+                    if pcs[2] == rank:
+                        exp["e" if c == 0 else late] += _relay_engines(topo, plan, h, rank)
+            for c in range(CH):
+                exp["e" if c == 0 else late] += sum(Q["per_dir"][c] for d in Q["direct"][c] if d[2] == rank)
 
     te.wait_ge(S.lf2, 16)
     te.wait_ge(S.own, 1)
-    te.wait_ge(S.arrs, exp["same"])
-    te.matmul(out=T.pc[:, 0:HB, :], lhsT=T.f2s[:], rhs=T.ls[:], start=True, stop=True).then_inc(S.y1, 1)
-    te.wait_ge(S.arrc, exp["cross"])
-    te.matmul(out=T.pd[:, 0:HB, :], lhsT=T.f2s[:], rhs=T.lc[:], start=True, stop=True).then_inc(S.y2, 1)
+    te.wait_ge(S.arre, exp["e"])
+    te.matmul(out=T.pe[:, 0:W, :, :], lhsT=T.f2s[:], rhs=T.land[:, a0:b0, :, :],
+              start=True, stop=True).then_inc(S.y0, 1)
+    te.wait_ge(S.arrs, exp["s"])
+    te.matmul(out=T.pc[:, 0:W, :], lhsT=T.f2s[:], rhs=T.land[:, a1:b1, ps, :],
+              start=True, stop=True).then_inc(S.y1, 1)
+    te.wait_ge(S.arrc, exp["c"])
+    te.matmul(out=T.pd[:, 0:W, :], lhsT=T.f2s[:], rhs=T.land[:, a1:b1, pc, :],
+              start=True, stop=True).then_inc(S.y2, 1)
+    ve.wait_ge(S.y0, 1)
+    ve.tensor_copy(out=T.ys[:, a0:b0, :, :], in_=T.pe[:, 0:W, :, :]).then_inc(S.cpe, 1)
     ve.wait_ge(S.y1, 1)
-    ve.tensor_copy(out=T.ys[:, :, ps, :], in_=T.pc[:, 0:HB, :]).then_inc(S.cp, 1)
+    ve.tensor_copy(out=T.ys[:, a1:b1, ps, :], in_=T.pc[:, 0:W, :]).then_inc(S.cp, 1)
     ve.wait_ge(S.y2, 1)
-    ve.tensor_copy(out=T.ys[:, :, pc, :], in_=T.pd[:, 0:HB, :]).then_inc(S.cp, 1)
+    ve.tensor_copy(out=T.ys[:, a1:b1, pc, :], in_=T.pd[:, 0:W, :]).then_inc(S.cp, 1)
+    g.sync.wait_ge(S.cpe, 1)
+    g.sync.dma_start(out=T.y[:, w * a0:w * b0], in_=T.ys[:, a0:b0, :, :]).then_inc(S.st, 16)
     g.sync.wait_ge(S.cp, 2)
-    g.sync.dma_start(out=T.y[:], in_=T.ys[:]).then_inc(S.st, 16)
-    g.sync.wait_ge(S.st, 16)
+    g.sync.dma_start(out=T.y[:, w * a1:w * b1], in_=T.ys[:, a1:b1, :, :]).then_inc(S.st, 16)
+    g.sync.wait_ge(S.st, 32)
     g.wait_ge(S.sent, sent)

from concourse.bass import DstId, RemoteDMATransfer
from concourse.mybir import AluOpType

N, TK = 16, 32
HB = N // 2
CH = 2
W = HB // CH

BF, F32 = "bfloat16", "float32"
SCRATCH = {
    "f1s": ("sbuf", [128, 128], BF),
    "f2s": ("sbuf", [128, 128], BF),
    "xs": ("sbuf", [128, HB, 2, TK], BF),
    "ts": ("sbuf", [128, HB, 2, TK], BF),
    "uc": ("sbuf", [128, HB, TK], BF),
    "us": ("sbuf", [128, HB, TK], BF),
    "hb0": ("sbuf", [128, TK], BF),
    "hb1": ("sbuf", [128, TK], BF),
    "land": ("sbuf", [128, HB, 2, TK], BF),
    "ys": ("sbuf", [128, HB, 2, TK], BF),
    "pe": ("psum", [128, HB, 2, TK], F32),
    "pc": ("psum", [128, N, TK], F32),
    "pd": ("psum", [128, N, TK], F32),
}
SEMAPHORES = ["lf1", "lf2", "own", "arre", "arrs", "arrc", "sent", "y0", "y1", "y2", "cpe", "cp", "st"]
for _c in range(CH):
    SCRATCH["pa%d" % _c] = ("psum", [128, N, TK], F32)
    SCRATCH["pb%d" % _c] = ("psum", [128, N, TK], F32)
    SEMAPHORES += ["lx%d" % _c, "lt%d" % _c, "mc%d" % _c, "ms%d" % _c, "uc%d" % _c, "ur%d" % _c, "o%d" % _c,
                   "got%d" % _c]


def _eng(topo, src, dst):
    m = topo.mask(src, dst)
    return [e for e in range(m.bit_length()) if (m >> e) & 1]


def _bits(es):
    return sum(1 << e for e in es)


def _pow2(n):
    p = 1
    while p * 2 <= n:
        p *= 2
    return p


def _ranges(idx):
    out = []
    for i in sorted(idx):
        if out and out[-1][1] == i:
            out[-1][1] = i + 1
        else:
            out.append([i, i + 1])
    return [tuple(r) for r in out]


def _plan(T, topo):
    cores = list(T.cores)
    n = len(cores)
    plan = []
    for j, R in enumerate(cores):
        ch = topo.chip(R)
        same = [r for r in range(n) if r == j or topo.same_plane(ch, topo.chip(cores[r]))]
        cross = [r for r in range(n) if r not in same]
        par_c, par_s = cross[0] % 2, same[0] % 2
        assert cross == [2 * i + par_c for i in range(HB)] and same == [2 * i + par_s for i in range(HB)]
        chip = [k for k in range(topo.CORES_PER_CHIP * topo.CHIPS) if topo.chip(k) == ch]
        away = lambda k: topo.die(k) != topo.die(R)
        port = sorted([k for k in chip if all(topo.may_write(k, cores[r]) for r in cross)],
                      key=lambda k: (away(k), k == R))
        rest = sorted([k for k in chip if k not in port and k != R], key=away)
        assert len(port) == W
        own = same.index(j)
        first = own // W
        half = [first] + [h for h in range(CH) if h != first]
        jobs = []
        direct = [[] for _ in range(CH)]
        off = []
        for k, h in enumerate(port):
            if h != R:
                jobs.append((h, [("uc", k + c * W, cross[k + c * W]) for c in half]))
            else:
                for p, c in enumerate(half):
                    direct[p].append(("uc", k + c * W, cross[k + c * W]))
                    off.append([i for i in range(c * W, (c + 1) * W) if i != own][0])
                jobs.append((rest.pop(0), [("us", s, same[s]) for s in off]))
        for p, c in enumerate(half):
            direct[p] += [("us", i, same[i]) for i in range(c * W, (c + 1) * W) if i != own and i not in off]
        far = _eng(topo, R, cores[cross[0]])
        on = _eng(topo, R, jobs[0][0])
        high = [e for e in on if e not in far] or on
        pools = [on, high]
        plan.append(dict(core=R, same=same, cross=cross, par_c=par_c, par_s=par_s, own=own, jobs=jobs,
                         direct=direct, off=off, pools=pools, half=half,
                         per_on=[_pow2(len(p) // len(jobs)) for p in pools],
                         per_dir=[_pow2(len(far) // len(d)) for d in direct]))
    return plan


def _send(g, T, topo, plan, j, core, items, per, local_sem, wave):
    trs = []
    for k, (src, r) in enumerate(items):
        P = plan[r]
        dst = P["core"]
        rid, pid, _ = topo.addr(dst)
        land = T.land[:, j // 2, j % 2, :]
        sem = T.sem.arre if wave == 0 else T.sem.arrc if j in P["cross"] else T.sem.arrs
        trs.append(RemoteDMATransfer(dst_ids=[DstId(rid=rid, pnc=pid)],
                                     dma_engine_mask=_bits(_eng(topo, core, dst)[k * per:(k + 1) * per]),
                                     remote_sem=sem, src=src, dst=land))
    g.remote_dma_fused(trs, local_sem=local_sem)
    return per * len(items)


def _relay_engines(topo, plan, helper, r):
    return _pow2(len(_eng(topo, helper, plan[r]["core"])))


def rank_program(g, core, T, topo):
    plan = _plan(T, topo)
    S = T.sem
    rank = T.rank_of(core)

    if rank is None:
        for j, P in enumerate(plan):
            for h, pieces in P["jobs"]:
                if h == core:
                    sent = 0
                    for c, (_, _, r) in enumerate(pieces):
                        g.wait_ge(S["got%d" % c], P["per_on"][c])
                        sent += _send(g, T, topo, plan, j, core, [(T["hb%d" % c][:], r)],
                                      _relay_engines(topo, plan, core, r), S.sent, c)
                    g.wait_ge(S.sent, sent)
        return

    P = plan[rank]
    pc, ps, own, off, half = P["par_c"], P["par_s"], P["own"], P["off"], P["half"]
    te, ve = g.tensor, g.vector
    mult = AluOpType.mult
    span = [(h * W, (h + 1) * W) for h in half]
    (a0, b0), (a1, b1) = span
    w = 2 * TK

    g.sync.dma_start(out=T.xs[:, a0:b0, :, :], in_=T.x[:, w * a0:w * b0]).then_inc(S.lx0, 16)
    g.scalar.dma_start(out=T.f1s[:], in_=T.f1[:]).then_inc(S.lf1, 16)
    g.scalar.dma_start(out=T.ts[:, a0:b0, :, :], in_=T.t[:, w * a0:w * b0]).then_inc(S.lt0, 16)
    g.scalar.dma_start(out=T.xs[:, a1:b1, :, :], in_=T.x[:, w * a1:w * b1]).then_inc(S.lx1, 16)
    g.scalar.dma_start(out=T.ts[:, a1:b1, :, :], in_=T.t[:, w * a1:w * b1]).then_inc(S.lt1, 16)
    g.scalar.dma_start(out=T.f2s[:], in_=T.f2[:]).then_inc(S.lf2, 16)

    te.wait_ge(S.lf1, 16)
    for c, (a, b) in enumerate(span):
        te.wait_ge(S["lx%d" % c], 16)
        te.matmul(out=T["pa%d" % c][:, 0:W, :], lhsT=T.f1s[:], rhs=T.xs[:, a:b, pc, :],
                  start=True, stop=True).then_inc(S["mc%d" % c], 1)
        te.matmul(out=T["pb%d" % c][:, 0:W, :], lhsT=T.f1s[:], rhs=T.xs[:, a:b, ps, :],
                  start=True, stop=True).then_inc(S["ms%d" % c], 1)

    def same_op(c, p, q, out, sem):
        a = span[c][0]
        ve.tensor_tensor(out=out, in0=T["pb%d" % c][:, p - a:q - a, :], in1=T.ts[:, p:q, ps, :],
                         op=mult).then_inc(sem, 1)

    nr = [0] * CH
    for c, (a, b) in enumerate(span):
        ve.wait_ge(S["lt%d" % c], 16)
        ve.wait_ge(S["mc%d" % c], 1)
        ve.tensor_tensor(out=T.uc[:, a:b, :], in0=T["pa%d" % c][:, 0:W, :], in1=T.ts[:, a:b, pc, :],
                         op=mult).then_inc(S["uc%d" % c], 1)
        ve.wait_ge(S["ms%d" % c], 1)
        if off:
            same_op(c, off[c], off[c] + 1, T.us[:, off[c]:off[c] + 1, :], S["o%d" % c])
        for p, q in _ranges([i for i in range(a, b) if i not in off]):
            same_op(c, p, q, T.us[:, p:q, :], S["ur%d" % c])
            nr[c] += 1
    same_op(0, own, own + 1, T.land[:, own:own + 1, ps, :], S.own)

    sent = 0
    for c in range(CH):
        g.wait_ge(S["uc%d" % c], 1)
        if off:
            g.wait_ge(S["o%d" % c], 1)
        per, pool = P["per_on"][c], P["pools"][c]
        trs = []
        for k, (h, pieces) in enumerate(P["jobs"]):
            buf, i, _ = pieces[c]
            rid, pid, _ = topo.addr(h)
            trs.append(RemoteDMATransfer(dst_ids=[DstId(rid=rid, pnc=pid)],
                                         dma_engine_mask=_bits(pool[k * per:(k + 1) * per]),
                                         remote_sem=S["got%d" % c], src=T[buf][:, i, :], dst=T["hb%d" % c][:]))
            sent += per
        g.remote_dma_fused(trs, local_sem=S.sent)
        g.wait_ge(S["ur%d" % c], nr[c])
        sent += _send(g, T, topo, plan, rank, core, [(T[buf][:, i, :], r) for buf, i, r in P["direct"][c]],
                      P["per_dir"][c], S.sent, c)

    exp = {"e": 0, "s": 0, "c": 0}
    for j, Q in enumerate(plan):
        if j != rank:
            late = "c" if j in P["cross"] else "s"
            for h, pieces in Q["jobs"]:
                for c, pcs in enumerate(pieces):
                    if pcs[2] == rank:
                        exp["e" if c == 0 else late] += _relay_engines(topo, plan, h, rank)
            for c in range(CH):
                exp["e" if c == 0 else late] += sum(Q["per_dir"][c] for d in Q["direct"][c] if d[2] == rank)

    te.wait_ge(S.lf2, 16)
    te.wait_ge(S.own, 1)
    te.wait_ge(S.arre, exp["e"])
    te.matmul(out=T.pe[:, 0:W, :, :], lhsT=T.f2s[:], rhs=T.land[:, a0:b0, :, :],
              start=True, stop=True).then_inc(S.y0, 1)
    te.wait_ge(S.arrs, exp["s"])
    te.matmul(out=T.pc[:, 0:W, :], lhsT=T.f2s[:], rhs=T.land[:, a1:b1, ps, :],
              start=True, stop=True).then_inc(S.y1, 1)
    te.wait_ge(S.arrc, exp["c"])
    te.matmul(out=T.pd[:, 0:W, :], lhsT=T.f2s[:], rhs=T.land[:, a1:b1, pc, :],
              start=True, stop=True).then_inc(S.y2, 1)
    ve.wait_ge(S.y0, 1)
    ve.tensor_copy(out=T.ys[:, a0:b0, :, :], in_=T.pe[:, 0:W, :, :]).then_inc(S.cpe, 1)
    ve.wait_ge(S.y1, 1)
    ve.tensor_copy(out=T.ys[:, a1:b1, ps, :], in_=T.pc[:, 0:W, :]).then_inc(S.cp, 1)
    ve.wait_ge(S.y2, 1)
    ve.tensor_copy(out=T.ys[:, a1:b1, pc, :], in_=T.pd[:, 0:W, :]).then_inc(S.cp, 1)
    g.sync.wait_ge(S.cpe, 1)
    g.sync.dma_start(out=T.y[:, w * a0:w * b0], in_=T.ys[:, a0:b0, :, :]).then_inc(S.st, 16)
    g.sync.wait_ge(S.cp, 2)
    g.sync.dma_start(out=T.y[:, w * a1:w * b1], in_=T.ys[:, a1:b1, :, :]).then_inc(S.st, 16)
    g.sync.wait_ge(S.st, 32)
    g.wait_ge(S.sent, sent)
